import numpy as np
import ml_dtypes


def mxq(x, axis, fmt="e4m3"):
    dtype, down = {"e4m3": (ml_dtypes.float8_e4m3fn, 7), "e5m2": (ml_dtypes.float8_e5m2, 14)}[fmt]
    v = np.moveaxis(np.asarray(x, np.float32).astype(ml_dtypes.bfloat16).astype(np.float64), axis, -1)
    blocks = v.reshape(v.shape[:-1] + (-1, 32))
    amax = np.abs(blocks).max(-1, keepdims=True)
    byte = np.maximum(np.where(amax > 0, np.frexp(amax)[1] - 1 + 127, 0) - down, 1)
    scale = np.exp2(byte - 127.0)
    codes = (blocks / scale).astype(np.float32).astype(dtype).astype(np.float64)
    return np.moveaxis((codes * scale).reshape(v.shape), -1, axis)


WIDE = False


def mx_kscale(k):
    if not WIDE:
        return np.ones(k)
    levels = np.array([10, -10, 5, -5, 0])
    if k % 512:
        return np.exp2(np.random.permutation(np.resize(levels, k // 32))).repeat(32)
    a = np.empty((k // 512, 16))
    for p in range(k // 512):
        a[p, :8] = np.random.permutation(np.resize(levels, 8))
        for g in range(8):
            far = levels[np.abs(levels - a[p, g]) >= 10]
            a[p, g + 8] = far[np.random.randint(len(far))]
    return np.exp2(a.ravel()).repeat(32)


def f64(x):
    return np.asarray(x).astype(np.float64)


def striped(idx):
    return np.tile(idx.reshape(-1, 16).T, (8, 1)).astype(np.uint16)


def unstriped(offs):
    return offs[:16].T.reshape(-1).astype(np.int64)


def striped8(idx):
    return np.concatenate([x.reshape(-1, 16).T for x in idx]).astype(np.uint16)


def runs(offs, k):
    lists = np.stack([offs[16 * r : 16 * r + 16].T.reshape(-1) for r in range(8)]).astype(np.int64)
    return lists[np.arange(k) % 512 // 64]


def pack_weight(w):
    k, n = w.shape
    w = f64(np.asarray(w, np.float32).astype(ml_dtypes.bfloat16)).reshape(k // 32, 32, n)
    amax = np.abs(w).max(1)
    byte = np.clip(np.where(amax > 0, np.frexp(amax)[1] - 1 + 127 - 7, 1), 1, 254)
    scaled = (w * np.exp2(127.0 - byte)[:, None, :]).reshape(k, n).astype(np.float32)
    words = np.ascontiguousarray(scaled.reshape(k // 512, 128, 4, n).transpose(0, 1, 3, 2)).astype(ml_dtypes.float8_e4m3fn).view(np.uint8)
    return words, np.ascontiguousarray(byte.astype(np.uint8).reshape(k // 512, 16, n))


def unpack_weight(words, scales):
    g, p, n, _ = words.shape
    vals = np.ascontiguousarray(words).view(ml_dtypes.float8_e4m3fn).astype(np.float64) * np.repeat(np.exp2(scales.astype(np.float64) - 127.0), 8, axis=1)[..., None]
    return vals.transpose(0, 1, 3, 2).reshape(g * 512, n)


E2M1 = np.array([0.0, 0.5, 1.0, 1.5, 2.0, 3.0, 4.0, 6.0, -0.0, -0.5, -1.0, -1.5, -2.0, -3.0, -4.0, -6.0])


def pack_fp4(w):
    k, n = w.shape
    w = f64(np.asarray(w, np.float32).astype(ml_dtypes.bfloat16)).reshape(k // 32, 32, n)
    amax = np.abs(w).max(1)
    mant, ex = np.frexp(amax / 6.0)
    byte = np.clip(np.where(amax > 0, np.where(mant > 0.5, ex, ex - 1) + 127, 1), 1, 254)
    scaled = (w * np.exp2(127.0 - byte)[:, None, :]).reshape(k, n).astype(np.float32)
    c = np.ascontiguousarray(scaled.reshape(k // 512, 128, 4, n).transpose(0, 1, 3, 2)).astype(ml_dtypes.float4_e2m1fn).view(np.uint8) & 0xF
    words = (c[..., 0::2] | (c[..., 1::2] << 4)).reshape(k // 512, 128, 2 * n)
    return np.ascontiguousarray(words), np.ascontiguousarray(byte.astype(np.uint8).reshape(k // 512, 16, n))


def unpack_fp4(words, scales):
    g, _, n = scales.shape
    words = np.ascontiguousarray(words).reshape(g, 128, n, 2)
    nib = np.empty((g, 128, n, 4), np.uint8)
    nib[..., 0::2] = words & 0xF
    nib[..., 1::2] = words >> 4
    vals = E2M1[nib] * np.repeat(np.exp2(scales.astype(np.float64) - 127.0), 8, axis=1)[..., None]
    return vals.transpose(0, 1, 3, 2).reshape(g * 512, n)


def relu(v):
    return np.maximum(v, 0.0)


K, T, S, H, G = 512, 1024, 256, 512, 2048


def setup_inputs():
    n = np.random.standard_normal
    s = mx_kscale(K)[:, None]
    packed_xT = pack_weight(n((K, T)) * s)
    packed_w1 = pack_fp4(n((K, H)) / np.sqrt(K) / s)
    packed_dT = pack_weight(n((K, G)) / s)
    return {
        "x_words": packed_xT[0],
        "x_scales": packed_xT[1],
        "w1_words": packed_w1[0],
        "w1_scales": packed_w1[1],
        "gs": (np.random.uniform(0.5, 1.5, (K, 1)) * s).astype(np.float32),
        "d_words": packed_dT[0],
        "d_scales": packed_dT[1],
        "offs": striped(np.random.permutation(T)[:S]),
        "n1": striped(np.random.permutation(S)),
        "n2": striped(np.random.permutation(S)),
        "k1": striped8(np.random.randint(0, G, (8, H))),
        "k2": striped8(np.random.randint(0, G, (8, H))),
        "two": striped(np.random.permutation(T)[:S]),
        "n3": striped(np.random.permutation(S)),
    }


def reference(x_words, x_scales, w1_words, w1_scales, gs, d_words, d_scales, offs, n1, n2, k1, k2, two, n3):
    d_k1 = unpack_weight(d_words, d_scales)[np.arange(K)[:, None], runs(k1, K)]
    xq = unpack_weight(x_words, x_scales)[:, unstriped(offs)]
    y = unpack_fp4(w1_words, w1_scales).T @ xq
    ds = np.zeros((H, S))
    ds[:, unstriped(n1)] = y
    z = f64(gs) * (np.maximum(y, ds[:, unstriped(n2)]))
    d_k2 = unpack_weight(d_words, d_scales)[np.arange(K)[:, None], runs(k2, K)]
    x_two = unpack_weight(x_words, x_scales)[:, unstriped(two)]
    h = 0.0625 * ((d_k1.T @ mxq(z, 0, "e4m3") + d_k2.T @ x_two))
    rl = relu(h)
    ds2 = np.zeros((H, S))
    ds2[:, unstriped(n3)] = rl
    return ds2 - (0.5 * h)

@@ -1,0 +1,218 @@
+from contextlib import ExitStack
+
+import concourse.mybir as mybir
+
+K, T, S, H, G = 512, 1024, 256, 512, 2048
+FLOPS = 3 * 2 * K * H * S
+
+F32 = mybir.dt.float32
+BF16 = mybir.dt.bfloat16
+I32 = mybir.dt.int32
+U32 = mybir.dt.uint32
+U16 = mybir.dt.uint16
+U8 = mybir.dt.uint8
+FP8X4 = mybir.dt.float8_e4m3fn_x4
+FP4X4 = mybir.dt.float4_e2m1fn_x4
+ALU = mybir.AluOpType
+ACT = mybir.ActivationFunctionType
+
+P = 128
+PACK = 4
+HALF = S // 2
+PER_COL = 16
+
+
+def entries(tile, first, count):
+    return tile[:, first // PER_COL : (first + count) // PER_COL]
+
+
+def tile_picked_cmixrelaysend_none_p_kernel(
+    tc, x_words, x_scales, w1_words, w1_scales, gs, d_words, d_scales, offs, n1, n2, k1, k2, two, n3, out
+):
+    nc = tc.nc
+    with ExitStack() as ctx:
+        lists = ctx.enter_context(tc.tile_pool(name="lists", bufs=1))
+        sb = ctx.enter_context(tc.tile_pool(name="sb", bufs=1))
+        psum = ctx.enter_context(tc.psum_pool(name="psum", bufs=1))
+
+        def load_list(name, src):
+            tile = lists.tile(list(src.shape), U16, name=name)
+            nc.sync.dma_start(tile[:], src)
+            return tile
+
+        def load_scale_rows(tile, src):
+            rows = src[0].bitcast(I32)
+            for q in range(4):
+                four = rows[4 * q : 4 * q + 4, :].rearrange("r c -> (r c)")
+                nc.sync.dma_start(tile[32 * q : 32 * q + 32, :].bitcast(I32), four.partition_broadcast(8))
+
+        xw = sb.tile([P, T], I32, name="xw", tag="xw", align_bytes=64)
+        xs = sb.tile([P, T], U8, name="xs", align_bytes=64)
+        w1w = sb.tile([P, 2 * H], U8, name="w1w", align_bytes=64)
+        w1s = sb.tile([P, H], U8, name="w1s", align_bytes=64)
+        dw = sb.tile([P, G], I32, name="dw", align_bytes=64)
+        dsc = sb.tile([P, G], U8, name="dsc", align_bytes=64)
+        gain = sb.tile([P, PACK], F32, name="gain")
+
+        offs_t = load_list("offs_t", offs)
+        nc.scalar.dma_start(xw[:], x_words[0].rearrange("p n t -> p (n t)").bitcast(I32))
+        nc.scalar.dma_start(w1w[:].bitcast(I32), w1_words[0].bitcast(I32))
+        load_scale_rows(xs, x_scales)
+        load_scale_rows(w1s, w1_scales)
+        n1_t = load_list("n1_t", n1)
+        nc.sync.dma_start(dsc[:].bitcast(I32), d_scales[0].bitcast(I32).unsqueeze(1).broadcast_to([16, 8, G // 4]))
+        k1_t = load_list("k1_t", k1)
+        k2_t = load_list("k2_t", k2)
+        nc.sync.dma_start(dw[:], d_words[0].rearrange("p n t -> p (n t)").bitcast(I32))
+        n2_t = load_list("n2_t", n2)
+        two_t = load_list("two_t", two)
+        nc.sync.dma_start(gain[:], gs.rearrange("(p t) o -> p (t o)", t=PACK))
+        n3_t = load_list("n3_t", n3)
+
+        dk_scales = sb.tile([P, 2 * H], U8, name="dk_scales", align_bytes=64)
+        nc.gpsimd.memset(dk_scales[:].bitcast(I32), 0)
+
+        w1w_d = sb.tile([P, 2 * H], U8, name="w1w_d", align_bytes=64)
+        w1s_d = sb.tile([P, H], U8, name="w1s_d", align_bytes=64)
+        nc.scalar.copy(
+            w1w_d[:].bitcast(U16).rearrange("p (t m) -> p t m", t=PACK),
+            w1w[:].bitcast(U16).rearrange("p (m t) -> p t m", t=PACK),
+        )
+        xq_s = sb.tile([P, S], U8, name="xq_s", align_bytes=64)
+        xq_w = sb.tile([P, S], U32, name="xq_w", align_bytes=64)
+        nc.vector.tensor_copy(xq_s[:], xs[:].indirect(offs_t[:]))
+        w1s_by_t = w1s[:].rearrange("p (m t) -> p t m", t=PACK)
+        w1s_d_by_t = w1s_d[:].rearrange("p (t m) -> p t m", t=PACK)
+        nc.vector.tensor_copy(w1s_d_by_t[:, 0, :], w1s_by_t[:, 0, :])
+
+        y_ps = [psum.tile([P, S], F32, name="y_ps%d" % t) for t in range(PACK)]
+        h_ps = [psum.tile([P, S], F32, name="h_ps%d" % t) for t in range(PACK)]
+        y_sb = [sb.tile([P, S], F32, name="y_sb%d" % t, tag="y_sb%d" % t) for t in range(PACK)]
+        ds = [sb.tile([P, 2 * S], F32, name="ds%d" % t) for t in range(PACK)]
+
+        def project(t, first, count):
+            cols = slice(first, first + count)
+            nc.tensor.matmul_mx(
+                out=y_ps[t][:, cols],
+                lhsT=w1w_d[:, 2 * P * t : 2 * P * (t + 1)].bitcast(FP4X4),
+                lhsT_scale=w1s_d[:, P * t : P * (t + 1)],
+                rhs=xq_w[:, cols].bitcast(FP8X4),
+                rhs_scale=xq_s[:, cols],
+                start=True,
+                stop=True,
+            )
+
+        def send_y(t, first, count):
+            nc.scalar.activation(ds[t][:].indirect(entries(n1_t, first, count)), y_sb[t][:, first : first + count], ACT.Copy)
+
+        nc.vector.tensor_copy(xq_w[:, :HALF], xw[:].bitcast(U32).indirect(entries(offs_t, 0, HALF)))
+        project(0, 0, HALF)
+        nc.scalar.activation(y_sb[0][:, :HALF], y_ps[0][:, :HALF], ACT.Copy)
+        send_y(0, 0, HALF)
+        nc.vector.tensor_copy(xq_w[:, HALF:], xw[:].bitcast(U32).indirect(entries(offs_t, HALF, HALF)))
+        project(0, HALF, HALF)
+        nc.vector.tensor_copy(w1s_d_by_t[:, 1:, :], w1s_by_t[:, 1:, :])
+        nc.vector.tensor_copy(y_sb[0][:, HALF:], y_ps[0][:, HALF:])
+        send_y(0, HALF, HALF)
+        for t in range(1, PACK):
+            project(t, 0, S)
+            nc.vector.tensor_copy(y_sb[t][:], y_ps[t][:])
+            send_y(t, 0, S)
+
+        dk_bytes = sb.tile([P, 2 * H], U8, name="dk_bytes", align_bytes=64)
+        nc.vector.tensor_copy(dk_bytes[:, :H], dsc[:].indirect(k1_t[:]))
+        nc.vector.tensor_copy(dk_bytes[:, H:], dsc[:].indirect(k2_t[:]))
+        for r in range(4):
+            nc.sync.dma_start(dk_scales[r:P:32, :].bitcast(I32), dk_bytes[8 * r : P : 32, :].bitcast(I32))
+
+        dk_lo = sb.tile([P, H], U32, name="dk_lo", align_bytes=64)
+        nc.vector.tensor_copy(dk_lo[:, : H // 2], dw[:].bitcast(U32).indirect(entries(k1_t, 0, H // 2)))
+        nc.vector.tensor_copy(dk_lo[:, H // 2 :], dw[:].bitcast(U32).indirect(entries(k2_t, 0, H // 2)))
+        x2_s = sb.tile([P, S], U8, name="x2_s", align_bytes=64)
+        x2_w = sb.tile([P, S], U32, name="x2_w", align_bytes=64)
+        nc.vector.tensor_copy(x2_s[:], xs[:].indirect(two_t[:]))
+        nc.vector.tensor_copy(x2_w[:], xw[:].bitcast(U32).indirect(two_t[:]))
+
+        z_w = sb.tile([P, S], U32, name="z_w", align_bytes=64)
+        z_s = sb.tile([P, S], U8, name="z_s", align_bytes=64)
+        fetched = [
+            sb.tile([P, PACK, HALF], F32, name="fetched0"),
+            sb.tile([P, PACK, HALF], F32, name="fetched1", tag="y_sb%d" % (PACK - 1)),
+        ]
+        larger = [
+            sb.tile([P, PACK, HALF], F32, name="larger0", tag="xw", align_bytes=64),
+            sb.tile([P, PACK, HALF], F32, name="larger1"),
+        ]
+        z_bf = [
+            sb.tile([P, HALF, PACK], BF16, name="z_bf0", align_bytes=64),
+            sb.tile([P, HALF, PACK], BF16, name="z_bf1", tag="z_bf1", align_bytes=64),
+        ]
+
+        def make_z(u):
+            cols = slice(u * HALF, (u + 1) * HALF)
+            for t in range(PACK):
+                nc.scalar.activation(fetched[u][:, t, :], ds[t][:, :S].indirect(entries(n2_t, u * HALF, HALF)), ACT.Copy)
+                nc.vector.tensor_tensor(larger[u][:, t, :], y_ps[t][:, cols], fetched[u][:, t, :], ALU.max)
+                nc.vector.tensor_scalar(z_bf[u][:, :, t], larger[u][:, t, :], gain[:, t : t + 1], None, ALU.mult)
+            nc.vector.quantize_mx(
+                out=z_w[:, cols].bitcast(FP8X4), scales=z_s[:, cols], in_=z_bf[u][:].rearrange("p c t -> p (c t)")
+            )
+
+        rl = [sb.tile([P, S], F32, name="rl%d" % t) for t in range(PACK)]
+        ds2 = [sb.tile([P, S if t < 2 else 2 * S], F32, name="ds2_%d" % t) for t in range(PACK)]
+
+        def mix(t, words, first, count):
+            cols = slice(first, first + count)
+            at = P * (t % 2)
+            nc.tensor.matmul_mx(
+                out=h_ps[t][:, cols],
+                lhsT=words[:, H // 2 + at : H // 2 + at + P].bitcast(FP8X4),
+                lhsT_scale=dk_scales[:, H + P * t : H + P * (t + 1)],
+                rhs=x2_w[:, cols].bitcast(FP8X4),
+                rhs_scale=x2_s[:, cols],
+                start=True,
+                stop=False,
+            )
+            nc.tensor.matmul_mx(
+                out=h_ps[t][:, cols],
+                lhsT=words[:, at : at + P].bitcast(FP8X4),
+                lhsT_scale=dk_scales[:, P * t : P * (t + 1)],
+                rhs=z_w[:, cols].bitcast(FP8X4),
+                rhs_scale=z_s[:, cols],
+                start=False,
+                stop=True,
+            )
+
+        def relu_on_vector(t, first, count):
+            cols = slice(first, first + count)
+            nc.vector.tensor_scalar(rl[t][:, cols], h_ps[t][:, cols], 0.0625, 0.0, ALU.mult, ALU.max)
+
+        def send_rl(t, first, count):
+            nc.scalar.activation(ds2[t][:].indirect(entries(n3_t, first, count)), rl[t][:, first : first + count], ACT.Copy)
+
+        def finish(t):
+            res = sb.tile([P, S], F32, name="res%d" % t)
+            nc.vector.scalar_tensor_tensor(res[:], h_ps[t][:], -0.5 * 0.0625, ds2[t][:, :S], ALU.mult, ALU.add)
+            nc.sync.dma_start(out[P * t : P * (t + 1), :], res[:])
+
+        make_z(0)
+        mix(0, dk_lo, 0, HALF)
+        mix(1, dk_lo, 0, HALF)
+        make_z(1)
+        nc.scalar.activation(rl[0][:, :HALF], h_ps[0][:, :HALF], ACT.Relu, scale=0.0625)
+        send_rl(0, 0, HALF)
+        relu_on_vector(1, 0, HALF)
+        send_rl(1, 0, HALF)
+        for t in range(2):
+            mix(t, dk_lo, HALF, HALF)
+            relu_on_vector(t, HALF, HALF)
+            send_rl(t, HALF, HALF)
+        dk_hi = sb.tile([P, H], U32, name="dk_hi", tag="z_bf1", align_bytes=64)
+        nc.vector.tensor_copy(dk_hi[:, : H // 2], dw[:].bitcast(U32).indirect(entries(k1_t, H // 2, H // 2)))
+        nc.vector.tensor_copy(dk_hi[:, H // 2 :], dw[:].bitcast(U32).indirect(entries(k2_t, H // 2, H // 2)))
+        for t in range(2, PACK):
+            mix(t, dk_hi, 0, S)
+            relu_on_vector(t, 0, S)
+            send_rl(t, 0, S)
+        for t in range(PACK):
+            finish(t)

@@ -40,46 +40,51 @@ def tile_picked_cmixrelaysend_none_p_kernel(
             nc.sync.dma_start(tile[:], src)
             return tile
 
-        def load_scale_rows(tile, src):
-            rows = src[0].bitcast(I32)
-            for q in range(4):
-                four = rows[4 * q : 4 * q + 4, :].rearrange("r c -> (r c)")
-                nc.sync.dma_start(tile[32 * q : 32 * q + 32, :].bitcast(I32), four.partition_broadcast(8))
+        def load_scale_rows(queue, tile, src, q):
+            four = src[0].bitcast(I32)[4 * q : 4 * q + 4, :].rearrange("r c -> (r c)")
+            queue.dma_start(tile[32 * q : 32 * q + 32, :].bitcast(I32), four.partition_broadcast(8))
 
-        xw = sb.tile([P, T], I32, name="xw", tag="xw", align_bytes=64)
+        xw = sb.tile([P, T], I32, name="xw", align_bytes=64)
         xs = sb.tile([P, T], U8, name="xs", align_bytes=64)
         w1w = sb.tile([P, 2 * H], U8, name="w1w", align_bytes=64)
         w1s = sb.tile([P, H], U8, name="w1s", align_bytes=64)
-        dw = sb.tile([P, G], I32, name="dw", align_bytes=64)
+        dw = sb.tile([P, G], I32, name="dw", tag="dw", align_bytes=64)
         dsc = sb.tile([P, G], U8, name="dsc", align_bytes=64)
         gain = sb.tile([P, PACK], F32, name="gain")
 
         offs_t = load_list("offs_t", offs)
-        nc.scalar.dma_start(xw[:], x_words[0].rearrange("p n t -> p (n t)").bitcast(I32))
+        load_scale_rows(nc.scalar, xs, x_scales, 0)
+        load_scale_rows(nc.sync, xs, x_scales, 1)
+        load_scale_rows(nc.scalar, xs, x_scales, 2)
+        nc.sync.dma_start(xw[:], x_words[0].rearrange("p n t -> p (n t)").bitcast(I32))
+        load_scale_rows(nc.scalar, xs, x_scales, 3)
+        load_scale_rows(nc.sync, w1s, w1_scales, 0)
         nc.scalar.dma_start(w1w[:].bitcast(I32), w1_words[0].bitcast(I32))
-        load_scale_rows(xs, x_scales)
-        load_scale_rows(w1s, w1_scales)
+        load_scale_rows(nc.sync, w1s, w1_scales, 1)
+        load_scale_rows(nc.scalar, w1s, w1_scales, 2)
+        load_scale_rows(nc.sync, w1s, w1_scales, 3)
         n1_t = load_list("n1_t", n1)
-        nc.sync.dma_start(dsc[:].bitcast(I32), d_scales[0].bitcast(I32).unsqueeze(1).broadcast_to([16, 8, G // 4]))
-        k1_t = load_list("k1_t", k1)
-        k2_t = load_list("k2_t", k2)
-        nc.sync.dma_start(dw[:], d_words[0].rearrange("p n t -> p (n t)").bitcast(I32))
-        n2_t = load_list("n2_t", n2)
         two_t = load_list("two_t", two)
+        k1_t = load_list("k1_t", k1)
+        nc.gpsimd.memset(dsc[:].bitcast(I32), 0)
+        nc.sync.dma_start(dsc[0:P:8, :].bitcast(I32), d_scales[0].bitcast(I32))
+        nc.sync.dma_start(dw[:], d_words[0].rearrange("p n t -> p (n t)").bitcast(I32))
+        k2_t = load_list("k2_t", k2)
+        n2_t = load_list("n2_t", n2)
         nc.sync.dma_start(gain[:], gs.rearrange("(p t) o -> p (t o)", t=PACK))
         n3_t = load_list("n3_t", n3)
 
         dk_scales = sb.tile([P, 2 * H], U8, name="dk_scales", align_bytes=64)
         nc.gpsimd.memset(dk_scales[:].bitcast(I32), 0)
 
-        w1w_d = sb.tile([P, 2 * H], U8, name="w1w_d", align_bytes=64)
+        w1w_d = sb.tile([P, 2 * H], U8, name="w1w_d", tag="w1w_d", align_bytes=64)
         w1s_d = sb.tile([P, H], U8, name="w1s_d", align_bytes=64)
         nc.scalar.copy(
             w1w_d[:].bitcast(U16).rearrange("p (t m) -> p t m", t=PACK),
             w1w[:].bitcast(U16).rearrange("p (m t) -> p t m", t=PACK),
         )
-        xq_s = sb.tile([P, S], U8, name="xq_s", align_bytes=64)
-        xq_w = sb.tile([P, S], U32, name="xq_w", align_bytes=64)
+        xq_s = sb.tile([P, S], U8, name="xq_s", tag="picked_s", align_bytes=64)
+        xq_w = sb.tile([P, S], U32, name="xq_w", tag="picked_w", align_bytes=64)
         nc.vector.tensor_copy(xq_s[:], xs[:].indirect(offs_t[:]))
         w1s_by_t = w1s[:].rearrange("p (m t) -> p t m", t=PACK)
         w1s_d_by_t = w1s_d[:].rearrange("p (t m) -> p t m", t=PACK)
@@ -119,66 +124,73 @@ def tile_picked_cmixrelaysend_none_p_kernel(
             nc.vector.tensor_copy(y_sb[t][:], y_ps[t][:])
             send_y(t, 0, S)
 
-        dk_bytes = sb.tile([P, 2 * H], U8, name="dk_bytes", align_bytes=64)
+        def pick_two(u, tag_s, tag_w):
+            scales = sb.tile([P, HALF], U8, name="x2_s%d" % u, tag=tag_s, align_bytes=64)
+            words = sb.tile([P, HALF], U32, name="x2_w%d" % u, tag=tag_w, align_bytes=64)
+            nc.vector.tensor_copy(scales[:], xs[:].indirect(entries(two_t, u * HALF, HALF)))
+            nc.vector.tensor_copy(words[:], xw[:].bitcast(U32).indirect(entries(two_t, u * HALF, HALF)))
+            return words, scales
+
+        x2 = [pick_two(0, "picked_s", "picked_w")]
+        dk_bytes = sb.tile([P, 2 * H], U8, name="dk_bytes", tag="w1w_d", align_bytes=64)
         nc.vector.tensor_copy(dk_bytes[:, :H], dsc[:].indirect(k1_t[:]))
         nc.vector.tensor_copy(dk_bytes[:, H:], dsc[:].indirect(k2_t[:]))
         for r in range(4):
             nc.sync.dma_start(dk_scales[r:P:32, :].bitcast(I32), dk_bytes[8 * r : P : 32, :].bitcast(I32))
 
-        dk_lo = sb.tile([P, H], U32, name="dk_lo", align_bytes=64)
-        nc.vector.tensor_copy(dk_lo[:, : H // 2], dw[:].bitcast(U32).indirect(entries(k1_t, 0, H // 2)))
-        nc.vector.tensor_copy(dk_lo[:, H // 2 :], dw[:].bitcast(U32).indirect(entries(k2_t, 0, H // 2)))
-        x2_s = sb.tile([P, S], U8, name="x2_s", align_bytes=64)
-        x2_w = sb.tile([P, S], U32, name="x2_w", align_bytes=64)
-        nc.vector.tensor_copy(x2_s[:], xs[:].indirect(two_t[:]))
-        nc.vector.tensor_copy(x2_w[:], xw[:].bitcast(U32).indirect(two_t[:]))
+        dk_words = sb.tile([P, 2 * H], U32, name="dk_words", align_bytes=64)
+        nc.vector.tensor_copy(dk_words[:, :H], dw[:].bitcast(U32).indirect(k1_t[:]))
+        nc.vector.tensor_copy(dk_words[:, H:], dw[:].bitcast(U32).indirect(k2_t[:]))
 
-        z_w = sb.tile([P, S], U32, name="z_w", align_bytes=64)
-        z_s = sb.tile([P, S], U8, name="z_s", align_bytes=64)
+        z_w = [sb.tile([P, HALF], U32, name="z_w%d" % u, tag="z_w%d" % u, align_bytes=64) for u in range(2)]
+        z_s = [sb.tile([P, HALF], U8, name="z_s%d" % u, tag="z_s%d" % u, align_bytes=64) for u in range(2)]
         fetched = [
             sb.tile([P, PACK, HALF], F32, name="fetched0"),
             sb.tile([P, PACK, HALF], F32, name="fetched1", tag="y_sb%d" % (PACK - 1)),
         ]
         larger = [
-            sb.tile([P, PACK, HALF], F32, name="larger0", tag="xw", align_bytes=64),
-            sb.tile([P, PACK, HALF], F32, name="larger1"),
+            sb.tile([P, PACK, HALF], F32, name="larger0", tag="dw", align_bytes=64),
+            None,
         ]
         z_bf = [
-            sb.tile([P, HALF, PACK], BF16, name="z_bf0", align_bytes=64),
-            sb.tile([P, HALF, PACK], BF16, name="z_bf1", tag="z_bf1", align_bytes=64),
+            sb.tile([P, HALF, PACK], BF16, name="z_bf0", tag="z_bf0", align_bytes=64),
+            sb.tile([P, HALF, PACK], BF16, name="z_bf1", align_bytes=64),
         ]
 
-        def make_z(u):
+        def fetch(u, t):
+            nc.scalar.activation(fetched[u][:, t, :], ds[t][:, :S].indirect(entries(n2_t, u * HALF, HALF)), ACT.Copy)
+
+        def weigh_and_quantise(u):
             cols = slice(u * HALF, (u + 1) * HALF)
-            for t in range(PACK):
-                nc.scalar.activation(fetched[u][:, t, :], ds[t][:, :S].indirect(entries(n2_t, u * HALF, HALF)), ACT.Copy)
-                nc.vector.tensor_tensor(larger[u][:, t, :], y_ps[t][:, cols], fetched[u][:, t, :], ALU.max)
-                nc.vector.tensor_scalar(z_bf[u][:, :, t], larger[u][:, t, :], gain[:, t : t + 1], None, ALU.mult)
+            for group in (range(PACK - 1), range(PACK - 1, PACK)):
+                for t in group:
+                    nc.vector.tensor_tensor(larger[u][:, t, :], y_ps[t][:, cols], fetched[u][:, t, :], ALU.max)
+                for t in group:
+                    nc.vector.tensor_scalar(z_bf[u][:, :, t], larger[u][:, t, :], gain[:, t : t + 1], None, ALU.mult)
             nc.vector.quantize_mx(
-                out=z_w[:, cols].bitcast(FP8X4), scales=z_s[:, cols], in_=z_bf[u][:].rearrange("p c t -> p (c t)")
+                out=z_w[u][:].bitcast(FP8X4), scales=z_s[u][:], in_=z_bf[u][:].rearrange("p c t -> p (c t)")
             )
 
         rl = [sb.tile([P, S], F32, name="rl%d" % t) for t in range(PACK)]
-        ds2 = [sb.tile([P, S if t < 2 else 2 * S], F32, name="ds2_%d" % t) for t in range(PACK)]
+        ds2 = [sb.tile([P, S], F32, name="ds2_%d" % t) for t in range(PACK)]
 
-        def mix(t, words, first, count):
-            cols = slice(first, first + count)
-            at = P * (t % 2)
+        def mix(t, u):
+            cols = slice(u * HALF, (u + 1) * HALF)
             nc.tensor.matmul_mx(
                 out=h_ps[t][:, cols],
-                lhsT=words[:, H // 2 + at : H // 2 + at + P].bitcast(FP8X4),
+                lhsT=dk_words[:, H + P * t : H + P * (t + 1)].bitcast(FP8X4),
                 lhsT_scale=dk_scales[:, H + P * t : H + P * (t + 1)],
-                rhs=x2_w[:, cols].bitcast(FP8X4),
-                rhs_scale=x2_s[:, cols],
+                rhs=x2[u][0][:].bitcast(FP8X4),
+                rhs_scale=x2[u][1][:],
                 start=True,
                 stop=False,
             )
             nc.tensor.matmul_mx(
                 out=h_ps[t][:, cols],
-                lhsT=words[:, at : at + P].bitcast(FP8X4),
+                lhsT=dk_words[:, P * t : P * (t + 1)].bitcast(FP8X4),
                 lhsT_scale=dk_scales[:, P * t : P * (t + 1)],
-                rhs=z_w[:, cols].bitcast(FP8X4),
-                rhs_scale=z_s[:, cols],
+                rhs=z_w[u][:].bitcast(FP8X4),
+                rhs_scale=z_s[u][:],
                 start=False,
                 stop=True,
             )
@@ -192,27 +204,27 @@ def tile_picked_cmixrelaysend_none_p_kernel(
 
         def finish(t):
             res = sb.tile([P, S], F32, name="res%d" % t)
-            nc.vector.scalar_tensor_tensor(res[:], h_ps[t][:], -0.5 * 0.0625, ds2[t][:, :S], ALU.mult, ALU.add)
+            nc.vector.scalar_tensor_tensor(res[:], h_ps[t][:], -0.5 * 0.0625, ds2[t][:], ALU.mult, ALU.add)
             nc.sync.dma_start(out[P * t : P * (t + 1), :], res[:])
 
-        make_z(0)
-        mix(0, dk_lo, 0, HALF)
-        mix(1, dk_lo, 0, HALF)
-        make_z(1)
+        for t in range(PACK):
+            fetch(0, t)
+        weigh_and_quantise(0)
+        for t in range(PACK):
+            mix(t, 0)
+        larger[1] = sb.tile([P, PACK, HALF], F32, name="larger1", tag="z_bf0", align_bytes=64)
+        for t in range(PACK):
+            fetch(1, t)
         nc.scalar.activation(rl[0][:, :HALF], h_ps[0][:, :HALF], ACT.Relu, scale=0.0625)
         send_rl(0, 0, HALF)
-        relu_on_vector(1, 0, HALF)
-        send_rl(1, 0, HALF)
-        for t in range(2):
-            mix(t, dk_lo, HALF, HALF)
+        for t in range(1, PACK):
+            relu_on_vector(t, 0, HALF)
+            send_rl(t, 0, HALF)
+        weigh_and_quantise(1)
+        x2.append(pick_two(1, "z_s0", "z_w0"))
+        for t in range(PACK):
+            mix(t, 1)
             relu_on_vector(t, HALF, HALF)
             send_rl(t, HALF, HALF)
-        dk_hi = sb.tile([P, H], U32, name="dk_hi", tag="z_bf1", align_bytes=64)
-        nc.vector.tensor_copy(dk_hi[:, : H // 2], dw[:].bitcast(U32).indirect(entries(k1_t, H // 2, H // 2)))
-        nc.vector.tensor_copy(dk_hi[:, H // 2 :], dw[:].bitcast(U32).indirect(entries(k2_t, H // 2, H // 2)))
-        for t in range(2, PACK):
-            mix(t, dk_hi, 0, S)
-            relu_on_vector(t, 0, S)
-            send_rl(t, 0, S)
         for t in range(PACK):
             finish(t)

from contextlib import ExitStack

import concourse.mybir as mybir

K, T, S, H, G = 512, 1024, 256, 512, 2048
FLOPS = 3 * 2 * K * H * S

F32 = mybir.dt.float32
BF16 = mybir.dt.bfloat16
I32 = mybir.dt.int32
U32 = mybir.dt.uint32
U16 = mybir.dt.uint16
U8 = mybir.dt.uint8
FP8X4 = mybir.dt.float8_e4m3fn_x4
FP4X4 = mybir.dt.float4_e2m1fn_x4
ALU = mybir.AluOpType
ACT = mybir.ActivationFunctionType

P = 128
PACK = 4
HALF = S // 2
PER_COL = 16


def entries(tile, first, count):
    return tile[:, first // PER_COL : (first + count) // PER_COL]


def tile_picked_cmixrelaysend_none_p_kernel(
    tc, x_words, x_scales, w1_words, w1_scales, gs, d_words, d_scales, offs, n1, n2, k1, k2, two, n3, out
):
    nc = tc.nc
    with ExitStack() as ctx:
        lists = ctx.enter_context(tc.tile_pool(name="lists", bufs=1))
        sb = ctx.enter_context(tc.tile_pool(name="sb", bufs=1))
        psum = ctx.enter_context(tc.psum_pool(name="psum", bufs=1))

        def load_list(name, src):
            tile = lists.tile(list(src.shape), U16, name=name)
            nc.sync.dma_start(tile[:], src)
            return tile

        def load_scale_rows(queue, tile, src, q):
            four = src[0].bitcast(I32)[4 * q : 4 * q + 4, :].rearrange("r c -> (r c)")
            queue.dma_start(tile[32 * q : 32 * q + 32, :].bitcast(I32), four.partition_broadcast(8))

        xw = sb.tile([P, T], I32, name="xw", align_bytes=64)
        xs = sb.tile([P, T], U8, name="xs", align_bytes=64)
        w1w = sb.tile([P, 2 * H], U8, name="w1w", align_bytes=64)
        w1s = sb.tile([P, H], U8, name="w1s", align_bytes=64)
        dw = sb.tile([P, G], I32, name="dw", tag="dw", align_bytes=64)
        dsc = sb.tile([P, G], U8, name="dsc", align_bytes=64)
        gain = sb.tile([P, PACK], F32, name="gain")

        offs_t = load_list("offs_t", offs)
        load_scale_rows(nc.scalar, xs, x_scales, 0)
        load_scale_rows(nc.sync, xs, x_scales, 1)
        load_scale_rows(nc.scalar, xs, x_scales, 2)
        nc.sync.dma_start(xw[:], x_words[0].rearrange("p n t -> p (n t)").bitcast(I32))
        load_scale_rows(nc.scalar, xs, x_scales, 3)
        load_scale_rows(nc.sync, w1s, w1_scales, 0)
        nc.scalar.dma_start(w1w[:].bitcast(I32), w1_words[0].bitcast(I32))
        load_scale_rows(nc.sync, w1s, w1_scales, 1)
        load_scale_rows(nc.scalar, w1s, w1_scales, 2)
        load_scale_rows(nc.sync, w1s, w1_scales, 3)
        n1_t = load_list("n1_t", n1)
        two_t = load_list("two_t", two)
        k1_t = load_list("k1_t", k1)
        nc.gpsimd.memset(dsc[:].bitcast(I32), 0)
        nc.sync.dma_start(dsc[0:P:8, :].bitcast(I32), d_scales[0].bitcast(I32))
        nc.sync.dma_start(dw[:], d_words[0].rearrange("p n t -> p (n t)").bitcast(I32))
        k2_t = load_list("k2_t", k2)
        n2_t = load_list("n2_t", n2)
        nc.sync.dma_start(gain[:], gs.rearrange("(p t) o -> p (t o)", t=PACK))
        n3_t = load_list("n3_t", n3)

        dk_scales = sb.tile([P, 2 * H], U8, name="dk_scales", align_bytes=64)
        nc.gpsimd.memset(dk_scales[:].bitcast(I32), 0)

        w1w_d = sb.tile([P, 2 * H], U8, name="w1w_d", tag="w1w_d", align_bytes=64)
        w1s_d = sb.tile([P, H], U8, name="w1s_d", align_bytes=64)
        nc.scalar.copy(
            w1w_d[:].bitcast(U16).rearrange("p (t m) -> p t m", t=PACK),
            w1w[:].bitcast(U16).rearrange("p (m t) -> p t m", t=PACK),
        )
        xq_s = sb.tile([P, S], U8, name="xq_s", tag="picked_s", align_bytes=64)
        xq_w = sb.tile([P, S], U32, name="xq_w", tag="picked_w", align_bytes=64)
        nc.vector.tensor_copy(xq_s[:], xs[:].indirect(offs_t[:]))
        w1s_by_t = w1s[:].rearrange("p (m t) -> p t m", t=PACK)
        w1s_d_by_t = w1s_d[:].rearrange("p (t m) -> p t m", t=PACK)
        nc.vector.tensor_copy(w1s_d_by_t[:, 0, :], w1s_by_t[:, 0, :])

        y_ps = [psum.tile([P, S], F32, name="y_ps%d" % t) for t in range(PACK)]
        h_ps = [psum.tile([P, S], F32, name="h_ps%d" % t) for t in range(PACK)]
        y_sb = [sb.tile([P, S], F32, name="y_sb%d" % t, tag="y_sb%d" % t) for t in range(PACK)]
        ds = [sb.tile([P, 2 * S], F32, name="ds%d" % t) for t in range(PACK)]

        def project(t, first, count):
            cols = slice(first, first + count)
            nc.tensor.matmul_mx(
                out=y_ps[t][:, cols],
                lhsT=w1w_d[:, 2 * P * t : 2 * P * (t + 1)].bitcast(FP4X4),
                lhsT_scale=w1s_d[:, P * t : P * (t + 1)],
                rhs=xq_w[:, cols].bitcast(FP8X4),
                rhs_scale=xq_s[:, cols],
                start=True,
                stop=True,
            )

        def send_y(t, first, count):
            nc.scalar.activation(ds[t][:].indirect(entries(n1_t, first, count)), y_sb[t][:, first : first + count], ACT.Copy)

        nc.vector.tensor_copy(xq_w[:, :HALF], xw[:].bitcast(U32).indirect(entries(offs_t, 0, HALF)))
        project(0, 0, HALF)
        nc.scalar.activation(y_sb[0][:, :HALF], y_ps[0][:, :HALF], ACT.Copy)
        send_y(0, 0, HALF)
        nc.vector.tensor_copy(xq_w[:, HALF:], xw[:].bitcast(U32).indirect(entries(offs_t, HALF, HALF)))
        project(0, HALF, HALF)
        nc.vector.tensor_copy(w1s_d_by_t[:, 1:, :], w1s_by_t[:, 1:, :])
        nc.vector.tensor_copy(y_sb[0][:, HALF:], y_ps[0][:, HALF:])
        send_y(0, HALF, HALF)
        for t in range(1, PACK):
            project(t, 0, S)
            nc.vector.tensor_copy(y_sb[t][:], y_ps[t][:])
            send_y(t, 0, S)

        def pick_two(u, tag_s, tag_w):
            scales = sb.tile([P, HALF], U8, name="x2_s%d" % u, tag=tag_s, align_bytes=64)
            words = sb.tile([P, HALF], U32, name="x2_w%d" % u, tag=tag_w, align_bytes=64)
            nc.vector.tensor_copy(scales[:], xs[:].indirect(entries(two_t, u * HALF, HALF)))
            nc.vector.tensor_copy(words[:], xw[:].bitcast(U32).indirect(entries(two_t, u * HALF, HALF)))
            return words, scales

        x2 = [pick_two(0, "picked_s", "picked_w")]
        dk_bytes = sb.tile([P, 2 * H], U8, name="dk_bytes", tag="w1w_d", align_bytes=64)
        nc.vector.tensor_copy(dk_bytes[:, :H], dsc[:].indirect(k1_t[:]))
        nc.vector.tensor_copy(dk_bytes[:, H:], dsc[:].indirect(k2_t[:]))
        for r in range(4):
            nc.sync.dma_start(dk_scales[r:P:32, :].bitcast(I32), dk_bytes[8 * r : P : 32, :].bitcast(I32))

        dk_words = sb.tile([P, 2 * H], U32, name="dk_words", align_bytes=64)
        nc.vector.tensor_copy(dk_words[:, :H], dw[:].bitcast(U32).indirect(k1_t[:]))
        nc.vector.tensor_copy(dk_words[:, H:], dw[:].bitcast(U32).indirect(k2_t[:]))

        z_w = [sb.tile([P, HALF], U32, name="z_w%d" % u, tag="z_w%d" % u, align_bytes=64) for u in range(2)]
        z_s = [sb.tile([P, HALF], U8, name="z_s%d" % u, tag="z_s%d" % u, align_bytes=64) for u in range(2)]
        fetched = [
            sb.tile([P, PACK, HALF], F32, name="fetched0"),
            sb.tile([P, PACK, HALF], F32, name="fetched1", tag="y_sb%d" % (PACK - 1)),
        ]
        larger = [
            sb.tile([P, PACK, HALF], F32, name="larger0", tag="dw", align_bytes=64),
            None,
        ]
        z_bf = [
            sb.tile([P, HALF, PACK], BF16, name="z_bf0", tag="z_bf0", align_bytes=64),
            sb.tile([P, HALF, PACK], BF16, name="z_bf1", align_bytes=64),
        ]

        def fetch(u, t):
            nc.scalar.activation(fetched[u][:, t, :], ds[t][:, :S].indirect(entries(n2_t, u * HALF, HALF)), ACT.Copy)

        def weigh_and_quantise(u):
            cols = slice(u * HALF, (u + 1) * HALF)
            for group in (range(PACK - 1), range(PACK - 1, PACK)):
                for t in group:
                    nc.vector.tensor_tensor(larger[u][:, t, :], y_ps[t][:, cols], fetched[u][:, t, :], ALU.max)
                for t in group:
                    nc.vector.tensor_scalar(z_bf[u][:, :, t], larger[u][:, t, :], gain[:, t : t + 1], None, ALU.mult)
            nc.vector.quantize_mx(
                out=z_w[u][:].bitcast(FP8X4), scales=z_s[u][:], in_=z_bf[u][:].rearrange("p c t -> p (c t)")
            )

        rl = [sb.tile([P, S], F32, name="rl%d" % t) for t in range(PACK)]
        ds2 = [sb.tile([P, S], F32, name="ds2_%d" % t) for t in range(PACK)]

        def mix(t, u):
            cols = slice(u * HALF, (u + 1) * HALF)
            nc.tensor.matmul_mx(
                out=h_ps[t][:, cols],
                lhsT=dk_words[:, H + P * t : H + P * (t + 1)].bitcast(FP8X4),
                lhsT_scale=dk_scales[:, H + P * t : H + P * (t + 1)],
                rhs=x2[u][0][:].bitcast(FP8X4),
                rhs_scale=x2[u][1][:],
                start=True,
                stop=False,
            )
            nc.tensor.matmul_mx(
                out=h_ps[t][:, cols],
                lhsT=dk_words[:, P * t : P * (t + 1)].bitcast(FP8X4),
                lhsT_scale=dk_scales[:, P * t : P * (t + 1)],
                rhs=z_w[u][:].bitcast(FP8X4),
                rhs_scale=z_s[u][:],
                start=False,
                stop=True,
            )

        def relu_on_vector(t, first, count):
            cols = slice(first, first + count)
            nc.vector.tensor_scalar(rl[t][:, cols], h_ps[t][:, cols], 0.0625, 0.0, ALU.mult, ALU.max)

        def send_rl(t, first, count):
            nc.scalar.activation(ds2[t][:].indirect(entries(n3_t, first, count)), rl[t][:, first : first + count], ACT.Copy)

        def finish(t):
            res = sb.tile([P, S], F32, name="res%d" % t)
            nc.vector.scalar_tensor_tensor(res[:], h_ps[t][:], -0.5 * 0.0625, ds2[t][:], ALU.mult, ALU.add)
            nc.sync.dma_start(out[P * t : P * (t + 1), :], res[:])

        for t in range(PACK):
            fetch(0, t)
        weigh_and_quantise(0)
        for t in range(PACK):
            mix(t, 0)
        larger[1] = sb.tile([P, PACK, HALF], F32, name="larger1", tag="z_bf0", align_bytes=64)
        for t in range(PACK):
            fetch(1, t)
        nc.scalar.activation(rl[0][:, :HALF], h_ps[0][:, :HALF], ACT.Relu, scale=0.0625)
        send_rl(0, 0, HALF)
        for t in range(1, PACK):
            relu_on_vector(t, 0, HALF)
            send_rl(t, 0, HALF)
        weigh_and_quantise(1)
        x2.append(pick_two(1, "z_s0", "z_w0"))
        for t in range(PACK):
            mix(t, 1)
            relu_on_vector(t, HALF, HALF)
            send_rl(t, HALF, HALF)
        for t in range(PACK):
            finish(t)
